import numpy as np
import ml_dtypes


def mxq(x, axis, fmt="e4m3"):
    dtype, down = {"e4m3": (ml_dtypes.float8_e4m3fn, 7), "e5m2": (ml_dtypes.float8_e5m2, 14)}[fmt]
    v = np.moveaxis(np.asarray(x, np.float32).astype(ml_dtypes.bfloat16).astype(np.float64), axis, -1)
    blocks = v.reshape(v.shape[:-1] + (-1, 32))
    amax = np.abs(blocks).max(-1, keepdims=True)
    byte = np.maximum(np.where(amax > 0, np.frexp(amax)[1] - 1 + 127, 0) - down, 1)
    scale = np.exp2(byte - 127.0)
    codes = (blocks / scale).astype(np.float32).astype(dtype).astype(np.float64)
    return np.moveaxis((codes * scale).reshape(v.shape), -1, axis)


WIDE = False


def mx_kscale(k):
    if not WIDE:
        return np.ones(k)
    levels = np.array([10, -10, 5, -5, 0])
    if k % 512:
        return np.exp2(np.random.permutation(np.resize(levels, k // 32))).repeat(32)
    a = np.empty((k // 512, 16))
    for p in range(k // 512):
        a[p, :8] = np.random.permutation(np.resize(levels, 8))
        for g in range(8):
            far = levels[np.abs(levels - a[p, g]) >= 10]
            a[p, g + 8] = far[np.random.randint(len(far))]
    return np.exp2(a.ravel()).repeat(32)


def f64(x):
    return np.asarray(x).astype(np.float64)


def striped(idx):
    return np.tile(idx.reshape(-1, 16).T, (8, 1)).astype(np.uint16)


def unstriped(offs):
    return offs[:16].T.reshape(-1).astype(np.int64)


E2M1 = np.array([0.0, 0.5, 1.0, 1.5, 2.0, 3.0, 4.0, 6.0, -0.0, -0.5, -1.0, -1.5, -2.0, -3.0, -4.0, -6.0])


def pack_weight(w, fmt):
    k, n = w.shape
    w = f64(np.asarray(w, np.float32).astype(ml_dtypes.bfloat16)).reshape(k // 32, 32, n)
    amax = np.abs(w).max(1)
    if fmt == "e4m3":
        byte = np.frexp(amax)[1] - 1 + 127 - 7
    else:
        mant, ex = np.frexp(amax / 6.0)
        byte = np.where(mant > 0.5, ex, ex - 1) + 127
    byte = np.clip(np.where(amax > 0, byte, 1), 1, 254)
    scaled = (w * np.exp2(127.0 - byte)[:, None, :]).reshape(k, n).astype(np.float32)
    by_word = np.ascontiguousarray(scaled.reshape(k // 512, 128, 4, n).transpose(0, 1, 3, 2))
    if fmt == "e4m3":
        words = by_word.astype(ml_dtypes.float8_e4m3fn).view(np.uint8)
    else:
        c = by_word.astype(ml_dtypes.float4_e2m1fn).view(np.uint8) & 0xF
        words = (c[..., 0::2] | (c[..., 1::2] << 4)).reshape(k // 512, 128, 2 * n)
    return np.ascontiguousarray(words), np.ascontiguousarray(byte.astype(np.uint8).reshape(k // 512, 16, n))


def unpack_weight(words, scales, fmt):
    g, _, n = scales.shape
    words = np.ascontiguousarray(words).reshape(g, 128, n, -1)
    if fmt == "e4m3":
        vals = words.view(ml_dtypes.float8_e4m3fn).astype(np.float64)
    else:
        nib = np.empty((g, 128, n, 4), np.uint8)
        nib[..., 0::2] = words & 0xF
        nib[..., 1::2] = words >> 4
        vals = E2M1[nib]
    vals = vals * np.repeat(np.exp2(scales.astype(np.float64) - 127.0), 8, axis=1)[..., None]
    return vals.transpose(0, 1, 3, 2).reshape(g * 512, n)


def gelu(v):
    return 0.5 * v * (1.0 + np.tanh(np.sqrt(2.0 / np.pi) * (v + 0.044715 * v**3)))


K, K1, K4, H, T, S, T3, S2 = 1536, 1024, 512, 1024, 2048, 512, 2048, 512

def setup_inputs():
    n = np.random.standard_normal
    s = mx_kscale(K)[:, None]
    u = mx_kscale(H)[:, None]
    tab_words, tab_scales = pack_weight(n((K, T)) * s, "e4m3")
    tab2_words, tab2_scales = pack_weight(n((H, T3)) / np.sqrt(H) / u, "e4m3")
    tab3_words, tab3_scales = pack_weight(n((H, T3)) / np.sqrt(H) / u, "e4m3")
    w4_words, w4_scales = pack_weight(1.2 * n((K4, H)) / np.sqrt(K) / s[K1:], "e2m1")
    return {
        "tab_words": tab_words, "tab_scales": tab_scales,
        "offs": striped(np.random.permutation(T)[:S]),
        "tab2_words": tab2_words, "tab2_scales": tab2_scales,
        "offs2": striped(np.random.permutation(T3)[:S2]),
        "tab3_words": tab3_words, "tab3_scales": tab3_scales,
        "offs3": striped(np.random.permutation(T3)[:S2]),
        "w1": (1.2 * n((K1, H)) / np.sqrt(K) / s[:K1]).astype(np.float32),
        "w4_words": w4_words, "w4_scales": w4_scales,
        "b1": (0.6 * n(H)).astype(np.float32),
        "gain": (1.5 * np.exp(0.3 * n(H)) * u[:, 0]).astype(np.float32),
    }

def reference(tab_words, tab_scales, offs, tab2_words, tab2_scales, offs2, tab3_words, tab3_scales, offs3, w1, w4_words, w4_scales, b1, gain):
    v = unpack_weight(tab_words, tab_scales, "e4m3")[:, unstriped(offs)]
    v2 = unpack_weight(tab2_words, tab2_scales, "e4m3")[:, unstriped(offs2)]
    v3 = unpack_weight(tab3_words, tab3_scales, "e4m3")[:, unstriped(offs3)]
    w1q = mxq(f64(w1), 0, "e4m3")
    w4 = unpack_weight(w4_words, w4_scales, "e2m1")
    x = (w1q.T @ v[:K1] + w4.T @ v[K1:]) + f64(b1)[:, None]
    gelu = 0.5 * x * (1.0 + np.tanh(0.7978845608 * (x + 0.044715 * x * x * x)))
    h = mxq(gelu * f64(gain)[:, None], 0, "e4m3")
    e2 = v2.T @ h
    e3 = v3.T @ h
    return np.tanh(e2) * np.exp(0.5 * e3)

@@ -1,0 +1,297 @@
+from contextlib import ExitStack
+
+import concourse.mybir as mybir
+
+F32 = mybir.dt.float32
+BF16 = mybir.dt.bfloat16
+I32 = mybir.dt.int32
+U32 = mybir.dt.uint32
+U16 = mybir.dt.uint16
+U8 = mybir.dt.uint8
+E4M3 = mybir.dt.float8_e4m3fn_x4
+E2M1 = mybir.dt.float4_e2m1fn_x4
+ACT = mybir.ActivationFunctionType
+MULT = mybir.AluOpType.mult
+
+P = 128
+T = 2048
+S = 512
+H = 1024
+HALF = S // 2
+FLOPS = 2 * S * (1536 * H + 2 * H * S)
+
+
+def tile_list_donor_hospital_shortlist_kernel(
+    tc, tab_words, tab_scales, offs, tab2_words, tab2_scales, offs2, tab3_words, tab3_scales, offs3,
+    w1, w4_words, w4_scales, b1, gain, out,
+):
+    nc = tc.nc
+    with ExitStack() as ctx:
+        sb = ctx.enter_context(tc.tile_pool(name="sb", bufs=1))
+        ps = ctx.enter_context(tc.psum_pool(name="ps", bufs=1))
+
+        def tile(name, shape, dtype, tag=None):
+            return sb.tile(shape, dtype, name=name, tag=tag or name, align_bytes=64)
+
+        def bank(n):
+            return ps.tile([P, S], F32, name="bank%d" % n, tag="bank%d" % n)
+
+        lists = {}
+
+        def load_list(name, src):
+            lists[name] = sb.tile([P, S // 16], U16, name=name)
+            nc.sync.dma_start(lists[name][:], src)
+
+        def load_words(name, words, a):
+            t = tile(name, [P, T], U32)
+            nc.sync.dma_start(t[:].bitcast(I32), words[a].rearrange("p n i -> p (n i)").bitcast(I32))
+            return t
+
+        def load_w1(a, b):
+            t = tile("w1raw%d%d" % (a, b), [P, 4, 512], F32)
+            nc.sync.dma_start(
+                t[:], w1[512 * a : 512 * (a + 1), 512 * b : 512 * (b + 1)].rearrange("(p j) c -> p j c", j=4)
+            )
+            return t
+
+        def load_planes(queue, dst, first_row, scales, a0, a1):
+            n = 4 * (a1 - a0)
+            for q in range(4):
+                r0 = 32 * q + first_row
+                src = scales[a0:a1, 4 * q : 4 * q + 4, :] if a1 - a0 > 1 else scales[a0, 4 * q : 4 * q + 4, :]
+                queue.dma_start(dst[r0 : r0 + n, :].bitcast(I32), src.bitcast(I32))
+
+        pat_planes = tile("pat_planes", [P, T], U8)
+        w4_planes_raw = tile("w4_planes_raw", [P, H], U8)
+        hos_planes = tile("hos_planes", [P, T], U8)
+        don_planes = tile("don_planes", [P, T], U8)
+        for t in (pat_planes, w4_planes_raw):
+            nc.vector.memset(t[:].bitcast(I32), 0)
+        for t in (hos_planes, don_planes):
+            nc.gpsimd.memset(t[:].bitcast(I32), 0)
+
+        raw = {}
+        w4_raw = tile("w4_raw", [P, 2 * H], U8)
+        nc.sync.dma_start(w4_raw[:].bitcast(I32), w4_words[0].bitcast(I32))
+        load_list("offs", offs)
+        load_planes(nc.sync, pat_planes, 4, tab_scales, 0, 2)
+        load_list("offs3", offs3)
+        raw[0, 0] = load_w1(0, 0)
+        load_planes(nc.sync, pat_planes, 0, tab_scales, 2, 3)
+        load_list("offs2", offs2)
+        pat = [load_words("pat0", tab_words, 0)]
+        load_planes(nc.sync, hos_planes, 0, tab3_scales, 0, 2)
+        raw[1, 0] = load_w1(1, 0)
+        load_planes(nc.sync, don_planes, 0, tab2_scales, 0, 2)
+        pat.append(load_words("pat1", tab_words, 1))
+        load_planes(nc.sync, w4_planes_raw, 0, w4_scales, 0, 1)
+        bias_t = tile("bias_t", [P, 2, 4], F32)
+        gain_t = [tile("gain_t%d" % b, [P, 4], F32) for b in range(2)]
+        nc.sync.dma_start(bias_t[:], b1.rearrange("(b p t) -> p b t", b=2, t=4))
+        pat.append(load_words("pat2", tab_words, 2))
+        raw[0, 1] = load_w1(0, 1)
+        nc.sync.dma_start(gain_t[0][:], gain[0:512].rearrange("(p t) -> p t", t=4))
+        raw[1, 1] = load_w1(1, 1)
+        hos = [load_words("hos%d" % a, tab3_words, a) for a in range(2)]
+        nc.sync.dma_start(gain_t[1][:], gain[512:1024].rearrange("(p t) -> p t", t=4))
+        don = [load_words("don%d" % a, tab2_words, a) for a in range(2)]
+
+        def gather(dst, window, name, first, count):
+            nc.vector.tensor_copy(
+                dst[:, first : first + count], window[:].indirect(lists[name][:, first // 16 : (first + count) // 16])
+            )
+
+        w1_bf, w1_codes, w1_scale = {}, {}, {}
+
+        def round_w1(engine_copy, a, b, th):
+            t = tile("w1bf%d%d%d" % (a, b, th), [P, 2, P, 4], BF16)
+            engine_copy(
+                t[:].rearrange("p t m j -> p m j t"),
+                raw[a, b][:].rearrange("p j (m t) -> p m j t", t=4)[:, :, :, 2 * th : 2 * th + 2],
+            )
+            w1_bf[a, b, th] = t
+
+        def quantize_w1(a, b, th):
+            c = tile("w1c%d%d%d" % (a, b, th), [P, 2 * P], U32)
+            s = tile("w1s%d%d%d" % (a, b, th), [P, 2 * P], U8)
+            nc.vector.quantize_mx(
+                c[:].bitcast(E4M3), s[:], w1_bf[a, b, th][:].rearrange("p t m j -> p (t m j)")
+            )
+            w1_codes[a, b, th], w1_scale[a, b, th] = c, s
+
+        pat_g = [tile("pat_g%d" % a, [P, S], U32) for a in range(3)]
+        pat_sg = tile("pat_sg", [P, S], U8)
+        pat_row = (4, 8, 0)
+        w4_codes = tile("w4_codes", [P, 2 * H], U8)
+        w4_scale = tile("w4_scale", [P, H], U8)
+
+        xbank = {}
+
+        def x_pass(b, a, jh, th, start, stop):
+            if start:
+                xbank[b, jh, th] = bank(4 * b + 2 * jh + th)
+            cols = slice(jh * HALF, (jh + 1) * HALF)
+            for ti in range(2):
+                if a < 2:
+                    lhs = w1_codes[a, b, th][:, ti * P : (ti + 1) * P].bitcast(E4M3)
+                    lhs_s = w1_scale[a, b, th][:, ti * P : (ti + 1) * P]
+                else:
+                    c0 = 512 * b + P * (2 * th + ti)
+                    lhs = w4_codes[:, 2 * c0 : 2 * (c0 + P)].bitcast(E2M1)
+                    lhs_s = w4_scale[:, c0 : c0 + P]
+                nc.tensor.matmul_mx(
+                    xbank[b, jh, th][:, ti * HALF : (ti + 1) * HALF],
+                    lhsT=lhs, lhsT_scale=lhs_s,
+                    rhs=pat_g[a][:, cols].bitcast(E4M3), rhs_scale=pat_sg[pat_row[a] :, cols],
+                    start=start and ti == 0, stop=stop and ti == 1,
+                )
+
+        act = {}
+
+        def gelu(b, jh):
+            g = tile("gelu%d%d" % (b, jh), [P, 4, HALF], F32)
+            for t in range(4):
+                nc.scalar.activation(
+                    g[:, t, :], xbank[b, jh, t // 2][:, (t % 2) * HALF : (t % 2 + 1) * HALF],
+                    ACT.Gelu_apprx_tanh, bias=bias_t[:, b, t : t + 1],
+                )
+            act[b, jh] = g
+
+        h_codes = {}
+        h_scale = [tile("h_scale%d" % b, [P, S], U8) for b in range(2)]
+        h_bf = {}
+
+        def scale_h(b, jh):
+            t = tile("hbf%d%d" % (b, jh), [P, HALF, 4], BF16)
+            nc.vector.tensor_tensor(
+                t[:].rearrange("p (c i) t -> p c t i", i=4),
+                act[b, jh][:].rearrange("p t (c i) -> p c t i", i=4),
+                gain_t[b][:].unsqueeze(1).unsqueeze(3).to_broadcast([P, HALF // 4, 4, 4]),
+                MULT,
+            )
+            h_bf[b, jh] = t
+
+        def quantize_h(b, jh):
+            cols = slice(jh * HALF, (jh + 1) * HALF)
+            nc.vector.quantize_mx(
+                h_codes[b][:, cols].bitcast(E4M3), h_scale[b][:, cols], h_bf[b, jh][:].rearrange("p j t -> p (j t)")
+            )
+
+        hos_g = [tile("hos_g%d" % a, [P, S], U32) for a in range(2)]
+        don_g = [tile("don_g%d" % a, [P, S], U32) for a in range(2)]
+        hos_sg = tile("hos_sg", [P, S], U8)
+        don_sg = tile("don_sg", [P, S], U8)
+        hos_bank, don_bank = {}, {}
+
+        def hos_pass(a, jh, mp):
+            if a == 0:
+                hos_bank[jh, mp] = bank(2 * jh + mp)
+            cols = slice(jh * HALF, (jh + 1) * HALF)
+            for mi in range(2):
+                m = slice((2 * mp + mi) * P, (2 * mp + mi + 1) * P)
+                nc.tensor.matmul_mx(
+                    hos_bank[jh, mp][:, mi * HALF : (mi + 1) * HALF],
+                    lhsT=hos_g[a][:, m].bitcast(E4M3), lhsT_scale=hos_sg[4 * a :, m],
+                    rhs=h_codes[a][:, cols].bitcast(E4M3), rhs_scale=h_scale[a][:, cols],
+                    start=a == 0 and mi == 0, stop=a == 1 and mi == 1,
+                )
+
+        def don_pass(a, mt):
+            if a == 0:
+                don_bank[mt] = bank(4 + mt)
+            m = slice(mt * P, (mt + 1) * P)
+            nc.tensor.matmul_mx(
+                don_bank[mt][:],
+                lhsT=don_g[a][:, m].bitcast(E4M3), lhsT_scale=don_sg[4 * a :, m],
+                rhs=h_codes[a][:].bitcast(E4M3), rhs_scale=h_scale[a][:],
+                start=a == 0, stop=a == 1,
+            )
+
+        hos_exp = tile("hos_exp", [P, 4, S], F32)
+
+        def exp_half(jh, mp):
+            nc.scalar.activation(
+                hos_exp[:, 2 * mp : 2 * mp + 2, jh * HALF : (jh + 1) * HALF],
+                hos_bank[jh, mp][:].rearrange("p (m j) -> p m j", m=2),
+                ACT.Exp, scale=0.5,
+            )
+
+        quads = [(jh, th) for jh in range(2) for th in range(2)]
+
+        nc.vector.tensor_copy(
+            w4_codes[:].bitcast(U16).rearrange("p (b t m) -> p b t m", b=2, t=4),
+            w4_raw[:].bitcast(U16).rearrange("p (b m t) -> p b t m", b=2, t=4),
+        )
+        gather(pat_sg, pat_planes, "offs", 0, S)
+        for th in range(2):
+            round_w1(nc.scalar.copy, 0, 0, th)
+            quantize_w1(0, 0, th)
+        gather(pat_g[0], pat[0], "offs", 0, S)
+        for jh, th in quads:
+            x_pass(0, 0, jh, th, True, False)
+        gather(hos_sg, hos_planes, "offs3", 0, S)
+        gather(don_sg, don_planes, "offs2", 0, S)
+        for th in range(2):
+            round_w1(nc.scalar.copy, 1, 0, th)
+            quantize_w1(1, 0, th)
+        gather(pat_g[1], pat[1], "offs", 0, S)
+        for jh, th in quads:
+            x_pass(0, 1, jh, th, False, False)
+        nc.vector.tensor_copy(
+            w4_scale[:].rearrange("p (b t m) -> p b t m", b=2, t=4),
+            w4_planes_raw[:].rearrange("p (b m t) -> p b t m", b=2, t=4),
+        )
+        for jh in range(2):
+            gather(pat_g[2], pat[2], "offs", jh * HALF, HALF)
+            for th in range(2):
+                x_pass(0, 2, jh, th, False, True)
+        for jh in range(2):
+            gelu(0, jh)
+        for jh, th in quads:
+            x_pass(1, 2, jh, th, True, False)
+
+        for th in range(2):
+            round_w1(nc.vector.tensor_copy, 0, 1, th)
+        for th in range(2):
+            round_w1(nc.scalar.copy, 1, 1, th)
+        for a in range(2):
+            for th in range(2):
+                quantize_w1(a, 1, th)
+        for jh in range(2):
+            scale_h(0, jh)
+        h_codes[0] = tile("h_codes0", [P, S], U32, tag="w1bf111")
+        h_codes[1] = tile("h_codes1", [P, S], U32)
+        for jh in range(2):
+            quantize_h(0, jh)
+        for a in range(2):
+            for jh, th in quads:
+                x_pass(1, a, jh, th, False, a == 1)
+        for jh in range(2):
+            gelu(1, jh)
+        gather(hos_g[0], hos[0], "offs3", 0, S)
+        for jh, mp in quads:
+            hos_pass(0, jh, mp)
+        gather(hos_g[1], hos[1], "offs3", 0, S)
+        scale_h(1, 0)
+        quantize_h(1, 0)
+        scale_h(1, 1)
+        for mp in range(2):
+            hos_pass(1, 0, mp)
+            exp_half(0, mp)
+        quantize_h(1, 1)
+        for mp in range(2):
+            hos_pass(1, 1, mp)
+            exp_half(1, mp)
+        for mp in range(2):
+            gather(don_g[0], don[0], "offs2", mp * HALF, HALF)
+            for mt in (2 * mp, 2 * mp + 1):
+                don_pass(0, mt)
+        for mt in range(4):
+            gather(don_g[1], don[1], "offs2", mt * P, P)
+            don_pass(1, mt)
+        for mt in range(4):
+            th_t = tile("tanh%d" % mt, [P, S], F32)
+            nc.scalar.activation(th_t[:], don_bank[mt][:], ACT.Tanh)
+            res = tile("res%d" % mt, [P, S], F32)
+            nc.vector.tensor_tensor(res[:], th_t[:], hos_exp[:, mt, :], MULT)
+            nc.sync.dma_start(out[mt * P : (mt + 1) * P, :], res[:])

@@ -18,6 +18,7 @@ T = 2048
 S = 512
 H = 1024
 HALF = S // 2
+HOS_ROW = 8
 FLOPS = 2 * S * (1536 * H + 2 * H * S)
 
 
@@ -65,30 +66,29 @@ def tile_list_donor_hospital_shortlist_kernel(
         w4_planes_raw = tile("w4_planes_raw", [P, H], U8)
         hos_planes = tile("hos_planes", [P, T], U8)
         don_planes = tile("don_planes", [P, T], U8)
-        for t in (pat_planes, w4_planes_raw):
+        for t in (pat_planes, w4_planes_raw, hos_planes, don_planes):
             nc.vector.memset(t[:].bitcast(I32), 0)
-        for t in (hos_planes, don_planes):
-            nc.gpsimd.memset(t[:].bitcast(I32), 0)
+
+        load_planes(nc.scalar, pat_planes, 0, tab_scales, 2, 3)
+        load_planes(nc.scalar, w4_planes_raw, 0, w4_scales, 0, 1)
+        load_planes(nc.gpsimd, pat_planes, 4, tab_scales, 0, 2)
+        load_planes(nc.gpsimd, hos_planes, HOS_ROW, tab3_scales, 0, 2)
+        load_planes(nc.gpsimd, don_planes, 0, tab2_scales, 0, 2)
 
         raw = {}
         w4_raw = tile("w4_raw", [P, 2 * H], U8)
         nc.sync.dma_start(w4_raw[:].bitcast(I32), w4_words[0].bitcast(I32))
         load_list("offs", offs)
-        load_planes(nc.sync, pat_planes, 4, tab_scales, 0, 2)
-        load_list("offs3", offs3)
         raw[0, 0] = load_w1(0, 0)
-        load_planes(nc.sync, pat_planes, 0, tab_scales, 2, 3)
-        load_list("offs2", offs2)
         pat = [load_words("pat0", tab_words, 0)]
-        load_planes(nc.sync, hos_planes, 0, tab3_scales, 0, 2)
+        load_list("offs3", offs3)
         raw[1, 0] = load_w1(1, 0)
-        load_planes(nc.sync, don_planes, 0, tab2_scales, 0, 2)
         pat.append(load_words("pat1", tab_words, 1))
-        load_planes(nc.sync, w4_planes_raw, 0, w4_scales, 0, 1)
         bias_t = tile("bias_t", [P, 2, 4], F32)
         gain_t = [tile("gain_t%d" % b, [P, 4], F32) for b in range(2)]
         nc.sync.dma_start(bias_t[:], b1.rearrange("(b p t) -> p b t", b=2, t=4))
         pat.append(load_words("pat2", tab_words, 2))
+        load_list("offs2", offs2)
         raw[0, 1] = load_w1(0, 1)
         nc.sync.dma_start(gain_t[0][:], gain[0:512].rearrange("(p t) -> p t", t=4))
         raw[1, 1] = load_w1(1, 1)
@@ -191,7 +191,7 @@ def tile_list_donor_hospital_shortlist_kernel(
                 m = slice((2 * mp + mi) * P, (2 * mp + mi + 1) * P)
                 nc.tensor.matmul_mx(
                     hos_bank[jh, mp][:, mi * HALF : (mi + 1) * HALF],
-                    lhsT=hos_g[a][:, m].bitcast(E4M3), lhsT_scale=hos_sg[4 * a :, m],
+                    lhsT=hos_g[a][:, m].bitcast(E4M3), lhsT_scale=hos_sg[HOS_ROW + 4 * a :, m],
                     rhs=h_codes[a][:, cols].bitcast(E4M3), rhs_scale=h_scale[a][:, cols],
                     start=a == 0 and mi == 0, stop=a == 1 and mi == 1,
                 )
@@ -222,6 +222,10 @@ def tile_list_donor_hospital_shortlist_kernel(
             w4_codes[:].bitcast(U16).rearrange("p (b t m) -> p b t m", b=2, t=4),
             w4_raw[:].bitcast(U16).rearrange("p (b m t) -> p b t m", b=2, t=4),
         )
+        nc.vector.tensor_copy(
+            w4_scale[:].rearrange("p (b t m) -> p b t m", b=2, t=4),
+            w4_planes_raw[:].rearrange("p (b m t) -> p b t m", b=2, t=4),
+        )
         gather(pat_sg, pat_planes, "offs", 0, S)
         for th in range(2):
             round_w1(nc.scalar.copy, 0, 0, th)
@@ -230,21 +234,17 @@ def tile_list_donor_hospital_shortlist_kernel(
         for jh, th in quads:
             x_pass(0, 0, jh, th, True, False)
         gather(hos_sg, hos_planes, "offs3", 0, S)
-        gather(don_sg, don_planes, "offs2", 0, S)
         for th in range(2):
             round_w1(nc.scalar.copy, 1, 0, th)
             quantize_w1(1, 0, th)
         gather(pat_g[1], pat[1], "offs", 0, S)
         for jh, th in quads:
             x_pass(0, 1, jh, th, False, False)
-        nc.vector.tensor_copy(
-            w4_scale[:].rearrange("p (b t m) -> p b t m", b=2, t=4),
-            w4_planes_raw[:].rearrange("p (b m t) -> p b t m", b=2, t=4),
-        )
         for jh in range(2):
             gather(pat_g[2], pat[2], "offs", jh * HALF, HALF)
             for th in range(2):
                 x_pass(0, 2, jh, th, False, True)
+        gather(don_sg, don_planes, "offs2", 0, S)
         for jh in range(2):
             gelu(0, jh)
         for jh, th in quads:

@@ -92,7 +92,7 @@ def tile_list_donor_hospital_shortlist_kernel(
         raw[0, 1] = load_w1(0, 1)
         nc.sync.dma_start(gain_t[0][:], gain[0:512].rearrange("(p t) -> p t", t=4))
         raw[1, 1] = load_w1(1, 1)
-        hos = [load_words("hos%d" % a, tab3_words, a) for a in range(2)]
+        hos = {a: load_words("hos%d" % a, tab3_words, a) for a in (1, 0)}
         nc.sync.dma_start(gain_t[1][:], gain[512:1024].rearrange("(p t) -> p t", t=4))
         don = [load_words("don%d" % a, tab2_words, a) for a in range(2)]
 
@@ -185,7 +185,7 @@ def tile_list_donor_hospital_shortlist_kernel(
 
         def hos_pass(a, jh, mp):
             if a == 0:
-                hos_bank[jh, mp] = bank(2 * jh + mp)
+                hos_bank[jh, mp] = bank(4 + 2 * jh + mp)
             cols = slice(jh * HALF, (jh + 1) * HALF)
             for mi in range(2):
                 m = slice((2 * mp + mi) * P, (2 * mp + mi + 1) * P)
@@ -198,7 +198,7 @@ def tile_list_donor_hospital_shortlist_kernel(
 
         def don_pass(a, mt):
             if a == 0:
-                don_bank[mt] = bank(4 + mt)
+                don_bank[mt] = bank(mt)
             m = slice(mt * P, (mt + 1) * P)
             nc.tensor.matmul_mx(
                 don_bank[mt][:],
@@ -268,10 +268,10 @@ def tile_list_donor_hospital_shortlist_kernel(
                 x_pass(1, a, jh, th, False, a == 1)
         for jh in range(2):
             gelu(1, jh)
-        gather(hos_g[0], hos[0], "offs3", 0, S)
+        for a in (1, 0):
+            gather(hos_g[a], hos[a], "offs3", 0, S)
         for jh, mp in quads:
             hos_pass(0, jh, mp)
-        gather(hos_g[1], hos[1], "offs3", 0, S)
         scale_h(1, 0)
         quantize_h(1, 0)
         scale_h(1, 1)
@@ -289,9 +289,9 @@ def tile_list_donor_hospital_shortlist_kernel(
         for mt in range(4):
             gather(don_g[1], don[1], "offs2", mt * P, P)
             don_pass(1, mt)
-        for mt in range(4):
-            th_t = tile("tanh%d" % mt, [P, S], F32)
-            nc.scalar.activation(th_t[:], don_bank[mt][:], ACT.Tanh)
-            res = tile("res%d" % mt, [P, S], F32)
-            nc.vector.tensor_tensor(res[:], th_t[:], hos_exp[:, mt, :], MULT)
-            nc.sync.dma_start(out[mt * P : (mt + 1) * P, :], res[:])
+        for mt, c0, c1 in ((0, 0, S), (1, 0, S), (2, 0, S), (3, 0, HALF), (3, HALF, S)):
+            th_t = tile("tanh%d_%d" % (mt, c0), [P, c1 - c0], F32)
+            nc.scalar.activation(th_t[:], don_bank[mt][:, c0:c1], ACT.Tanh)
+            res = tile("res%d_%d" % (mt, c0), [P, c1 - c0], F32)
+            nc.vector.tensor_tensor(res[:], th_t[:], hos_exp[:, mt, c0:c1], MULT)
+            nc.sync.dma_start(out[mt * P : (mt + 1) * P, c0:c1], res[:])

from contextlib import ExitStack

import concourse.mybir as mybir

F32 = mybir.dt.float32
BF16 = mybir.dt.bfloat16
I32 = mybir.dt.int32
U32 = mybir.dt.uint32
U16 = mybir.dt.uint16
U8 = mybir.dt.uint8
E4M3 = mybir.dt.float8_e4m3fn_x4
E2M1 = mybir.dt.float4_e2m1fn_x4
ACT = mybir.ActivationFunctionType
MULT = mybir.AluOpType.mult

P = 128
T = 2048
S = 512
H = 1024
HALF = S // 2
HOS_ROW = 8
FLOPS = 2 * S * (1536 * H + 2 * H * S)


def tile_list_donor_hospital_shortlist_kernel(
    tc, tab_words, tab_scales, offs, tab2_words, tab2_scales, offs2, tab3_words, tab3_scales, offs3,
    w1, w4_words, w4_scales, b1, gain, out,
):
    nc = tc.nc
    with ExitStack() as ctx:
        sb = ctx.enter_context(tc.tile_pool(name="sb", bufs=1))
        ps = ctx.enter_context(tc.psum_pool(name="ps", bufs=1))

        def tile(name, shape, dtype, tag=None):
            return sb.tile(shape, dtype, name=name, tag=tag or name, align_bytes=64)

        def bank(n):
            return ps.tile([P, S], F32, name="bank%d" % n, tag="bank%d" % n)

        lists = {}

        def load_list(name, src):
            lists[name] = sb.tile([P, S // 16], U16, name=name)
            nc.sync.dma_start(lists[name][:], src)

        def load_words(name, words, a):
            t = tile(name, [P, T], U32)
            nc.sync.dma_start(t[:].bitcast(I32), words[a].rearrange("p n i -> p (n i)").bitcast(I32))
            return t

        def load_w1(a, b):
            t = tile("w1raw%d%d" % (a, b), [P, 4, 512], F32)
            nc.sync.dma_start(
                t[:], w1[512 * a : 512 * (a + 1), 512 * b : 512 * (b + 1)].rearrange("(p j) c -> p j c", j=4)
            )
            return t

        def load_planes(queue, dst, first_row, scales, a0, a1):
            n = 4 * (a1 - a0)
            for q in range(4):
                r0 = 32 * q + first_row
                src = scales[a0:a1, 4 * q : 4 * q + 4, :] if a1 - a0 > 1 else scales[a0, 4 * q : 4 * q + 4, :]
                queue.dma_start(dst[r0 : r0 + n, :].bitcast(I32), src.bitcast(I32))

        pat_planes = tile("pat_planes", [P, T], U8)
        w4_planes_raw = tile("w4_planes_raw", [P, H], U8)
        hos_planes = tile("hos_planes", [P, T], U8)
        don_planes = tile("don_planes", [P, T], U8)
        for t in (pat_planes, w4_planes_raw, hos_planes, don_planes):
            nc.vector.memset(t[:].bitcast(I32), 0)

        load_planes(nc.scalar, pat_planes, 0, tab_scales, 2, 3)
        load_planes(nc.scalar, w4_planes_raw, 0, w4_scales, 0, 1)
        load_planes(nc.gpsimd, pat_planes, 4, tab_scales, 0, 2)
        load_planes(nc.gpsimd, hos_planes, HOS_ROW, tab3_scales, 0, 2)
        load_planes(nc.gpsimd, don_planes, 0, tab2_scales, 0, 2)

        raw = {}
        w4_raw = tile("w4_raw", [P, 2 * H], U8)
        nc.sync.dma_start(w4_raw[:].bitcast(I32), w4_words[0].bitcast(I32))
        load_list("offs", offs)
        raw[0, 0] = load_w1(0, 0)
        pat = [load_words("pat0", tab_words, 0)]
        load_list("offs3", offs3)
        raw[1, 0] = load_w1(1, 0)
        pat.append(load_words("pat1", tab_words, 1))
        bias_t = tile("bias_t", [P, 2, 4], F32)
        gain_t = [tile("gain_t%d" % b, [P, 4], F32) for b in range(2)]
        nc.sync.dma_start(bias_t[:], b1.rearrange("(b p t) -> p b t", b=2, t=4))
        pat.append(load_words("pat2", tab_words, 2))
        load_list("offs2", offs2)
        raw[0, 1] = load_w1(0, 1)
        nc.sync.dma_start(gain_t[0][:], gain[0:512].rearrange("(p t) -> p t", t=4))
        raw[1, 1] = load_w1(1, 1)
        hos = {a: load_words("hos%d" % a, tab3_words, a) for a in (1, 0)}
        nc.sync.dma_start(gain_t[1][:], gain[512:1024].rearrange("(p t) -> p t", t=4))
        don = [load_words("don%d" % a, tab2_words, a) for a in range(2)]

        def gather(dst, window, name, first, count):
            nc.vector.tensor_copy(
                dst[:, first : first + count], window[:].indirect(lists[name][:, first // 16 : (first + count) // 16])
            )

        w1_bf, w1_codes, w1_scale = {}, {}, {}

        def round_w1(engine_copy, a, b, th):
            t = tile("w1bf%d%d%d" % (a, b, th), [P, 2, P, 4], BF16)
            engine_copy(
                t[:].rearrange("p t m j -> p m j t"),
                raw[a, b][:].rearrange("p j (m t) -> p m j t", t=4)[:, :, :, 2 * th : 2 * th + 2],
            )
            w1_bf[a, b, th] = t

        def quantize_w1(a, b, th):
            c = tile("w1c%d%d%d" % (a, b, th), [P, 2 * P], U32)
            s = tile("w1s%d%d%d" % (a, b, th), [P, 2 * P], U8)
            nc.vector.quantize_mx(
                c[:].bitcast(E4M3), s[:], w1_bf[a, b, th][:].rearrange("p t m j -> p (t m j)")
            )
            w1_codes[a, b, th], w1_scale[a, b, th] = c, s

        pat_g = [tile("pat_g%d" % a, [P, S], U32) for a in range(3)]
        pat_sg = tile("pat_sg", [P, S], U8)
        pat_row = (4, 8, 0)
        w4_codes = tile("w4_codes", [P, 2 * H], U8)
        w4_scale = tile("w4_scale", [P, H], U8)

        xbank = {}

        def x_pass(b, a, jh, th, start, stop):
            if start:
                xbank[b, jh, th] = bank(4 * b + 2 * jh + th)
            cols = slice(jh * HALF, (jh + 1) * HALF)
            for ti in range(2):
                if a < 2:
                    lhs = w1_codes[a, b, th][:, ti * P : (ti + 1) * P].bitcast(E4M3)
                    lhs_s = w1_scale[a, b, th][:, ti * P : (ti + 1) * P]
                else:
                    c0 = 512 * b + P * (2 * th + ti)
                    lhs = w4_codes[:, 2 * c0 : 2 * (c0 + P)].bitcast(E2M1)
                    lhs_s = w4_scale[:, c0 : c0 + P]
                nc.tensor.matmul_mx(
                    xbank[b, jh, th][:, ti * HALF : (ti + 1) * HALF],
                    lhsT=lhs, lhsT_scale=lhs_s,
                    rhs=pat_g[a][:, cols].bitcast(E4M3), rhs_scale=pat_sg[pat_row[a] :, cols],
                    start=start and ti == 0, stop=stop and ti == 1,
                )

        act = {}

        def gelu(b, jh):
            g = tile("gelu%d%d" % (b, jh), [P, 4, HALF], F32)
            for t in range(4):
                nc.scalar.activation(
                    g[:, t, :], xbank[b, jh, t // 2][:, (t % 2) * HALF : (t % 2 + 1) * HALF],
                    ACT.Gelu_apprx_tanh, bias=bias_t[:, b, t : t + 1],
                )
            act[b, jh] = g

        h_codes = {}
        h_scale = [tile("h_scale%d" % b, [P, S], U8) for b in range(2)]
        h_bf = {}

        def scale_h(b, jh):
            t = tile("hbf%d%d" % (b, jh), [P, HALF, 4], BF16)
            nc.vector.tensor_tensor(
                t[:].rearrange("p (c i) t -> p c t i", i=4),
                act[b, jh][:].rearrange("p t (c i) -> p c t i", i=4),
                gain_t[b][:].unsqueeze(1).unsqueeze(3).to_broadcast([P, HALF // 4, 4, 4]),
                MULT,
            )
            h_bf[b, jh] = t

        def quantize_h(b, jh):
            cols = slice(jh * HALF, (jh + 1) * HALF)
            nc.vector.quantize_mx(
                h_codes[b][:, cols].bitcast(E4M3), h_scale[b][:, cols], h_bf[b, jh][:].rearrange("p j t -> p (j t)")
            )

        hos_g = [tile("hos_g%d" % a, [P, S], U32) for a in range(2)]
        don_g = [tile("don_g%d" % a, [P, S], U32) for a in range(2)]
        hos_sg = tile("hos_sg", [P, S], U8)
        don_sg = tile("don_sg", [P, S], U8)
        hos_bank, don_bank = {}, {}

        def hos_pass(a, jh, mp):
            if a == 0:
                hos_bank[jh, mp] = bank(4 + 2 * jh + mp)
            cols = slice(jh * HALF, (jh + 1) * HALF)
            for mi in range(2):
                m = slice((2 * mp + mi) * P, (2 * mp + mi + 1) * P)
                nc.tensor.matmul_mx(
                    hos_bank[jh, mp][:, mi * HALF : (mi + 1) * HALF],
                    lhsT=hos_g[a][:, m].bitcast(E4M3), lhsT_scale=hos_sg[HOS_ROW + 4 * a :, m],
                    rhs=h_codes[a][:, cols].bitcast(E4M3), rhs_scale=h_scale[a][:, cols],
                    start=a == 0 and mi == 0, stop=a == 1 and mi == 1,
                )

        def don_pass(a, mt):
            if a == 0:
                don_bank[mt] = bank(mt)
            m = slice(mt * P, (mt + 1) * P)
            nc.tensor.matmul_mx(
                don_bank[mt][:],
                lhsT=don_g[a][:, m].bitcast(E4M3), lhsT_scale=don_sg[4 * a :, m],
                rhs=h_codes[a][:].bitcast(E4M3), rhs_scale=h_scale[a][:],
                start=a == 0, stop=a == 1,
            )

        hos_exp = tile("hos_exp", [P, 4, S], F32)

        def exp_half(jh, mp):
            nc.scalar.activation(
                hos_exp[:, 2 * mp : 2 * mp + 2, jh * HALF : (jh + 1) * HALF],
                hos_bank[jh, mp][:].rearrange("p (m j) -> p m j", m=2),
                ACT.Exp, scale=0.5,
            )

        quads = [(jh, th) for jh in range(2) for th in range(2)]

        nc.vector.tensor_copy(
            w4_codes[:].bitcast(U16).rearrange("p (b t m) -> p b t m", b=2, t=4),
            w4_raw[:].bitcast(U16).rearrange("p (b m t) -> p b t m", b=2, t=4),
        )
        nc.vector.tensor_copy(
            w4_scale[:].rearrange("p (b t m) -> p b t m", b=2, t=4),
            w4_planes_raw[:].rearrange("p (b m t) -> p b t m", b=2, t=4),
        )
        gather(pat_sg, pat_planes, "offs", 0, S)
        for th in range(2):
            round_w1(nc.scalar.copy, 0, 0, th)
            quantize_w1(0, 0, th)
        gather(pat_g[0], pat[0], "offs", 0, S)
        for jh, th in quads:
            x_pass(0, 0, jh, th, True, False)
        gather(hos_sg, hos_planes, "offs3", 0, S)
        for th in range(2):
            round_w1(nc.scalar.copy, 1, 0, th)
            quantize_w1(1, 0, th)
        gather(pat_g[1], pat[1], "offs", 0, S)
        for jh, th in quads:
            x_pass(0, 1, jh, th, False, False)
        for jh in range(2):
            gather(pat_g[2], pat[2], "offs", jh * HALF, HALF)
            for th in range(2):
                x_pass(0, 2, jh, th, False, True)
        gather(don_sg, don_planes, "offs2", 0, S)
        for jh in range(2):
            gelu(0, jh)
        for jh, th in quads:
            x_pass(1, 2, jh, th, True, False)

        for th in range(2):
            round_w1(nc.vector.tensor_copy, 0, 1, th)
        for th in range(2):
            round_w1(nc.scalar.copy, 1, 1, th)
        for a in range(2):
            for th in range(2):
                quantize_w1(a, 1, th)
        for jh in range(2):
            scale_h(0, jh)
        h_codes[0] = tile("h_codes0", [P, S], U32, tag="w1bf111")
        h_codes[1] = tile("h_codes1", [P, S], U32)
        for jh in range(2):
            quantize_h(0, jh)
        for a in range(2):
            for jh, th in quads:
                x_pass(1, a, jh, th, False, a == 1)
        for jh in range(2):
            gelu(1, jh)
        for a in (1, 0):
            gather(hos_g[a], hos[a], "offs3", 0, S)
        for jh, mp in quads:
            hos_pass(0, jh, mp)
        scale_h(1, 0)
        quantize_h(1, 0)
        scale_h(1, 1)
        for mp in range(2):
            hos_pass(1, 0, mp)
            exp_half(0, mp)
        quantize_h(1, 1)
        for mp in range(2):
            hos_pass(1, 1, mp)
            exp_half(1, mp)
        for mp in range(2):
            gather(don_g[0], don[0], "offs2", mp * HALF, HALF)
            for mt in (2 * mp, 2 * mp + 1):
                don_pass(0, mt)
        for mt in range(4):
            gather(don_g[1], don[1], "offs2", mt * P, P)
            don_pass(1, mt)
        for mt, c0, c1 in ((0, 0, S), (1, 0, S), (2, 0, S), (3, 0, HALF), (3, HALF, S)):
            th_t = tile("tanh%d_%d" % (mt, c0), [P, c1 - c0], F32)
            nc.scalar.activation(th_t[:], don_bank[mt][:, c0:c1], ACT.Tanh)
            res = tile("res%d_%d" % (mt, c0), [P, c1 - c0], F32)
            nc.vector.tensor_tensor(res[:], th_t[:], hos_exp[:, mt, c0:c1], MULT)
            nc.sync.dma_start(out[mt * P : (mt + 1) * P, c0:c1], res[:])
